import numpy as np
import ml_dtypes

BF16 = ml_dtypes.bfloat16


def bf(x):
    return np.asarray(x, np.float32).astype(BF16)


def f32(x):
    return np.asarray(x, np.float32)


def f64(x):
    return np.asarray(x).astype(np.float64)


def striped(idx):
    return np.tile(idx.reshape(-1, 16).T, (8, 1))


S, K, M, N, D, V = 256, 128, 512, 256, 2, 128


def setup_inputs():
    return {"table": bf(np.random.standard_normal((K, S))), "w": bf(np.random.standard_normal((K, M)) / np.sqrt(D * K)), "b": f32(0.5 * np.random.standard_normal((M, 1))), "offs": striped(np.random.permutation(np.tile(np.arange(S), 2))[:N])}


def reference(table, w, b, offs):
    idx = offs[:16].T.reshape(-1)
    x = f64(table)[:, idx]
    y = f64(w).T @ sum(x[:, t * V : (t + 1) * V] for t in range(D))
    return np.maximum(y + f64(b), 0.0)

@@ -1,0 +1,41 @@
+import concourse.mybir as mybir
+
+P = 128
+M = 512
+V = 128
+T = 2
+BLOCKS = M // P
+PIECE = V // 16
+
+FLOPS = 2 * P * M * V * T
+
+
+def tile_gather_matmul_kernel(tc, table, w, b, offs, out):
+    nc = tc.nc
+    f32, bf16, u16 = mybir.dt.float32, mybir.dt.bfloat16, mybir.dt.uint16
+    add, largest = mybir.AluOpType.add, mybir.AluOpType.max
+    nodes = table.shape[1]
+
+    with (
+        tc.tile_pool(name="held", bufs=1) as held,
+        tc.psum_pool(name="sums", bufs=BLOCKS) as sums,
+    ):
+        offsets = held.tile([P, T * PIECE], u16, name="offsets")
+        nc.sync.dma_start(offsets[:], offs)
+        features = held.tile([P, nodes], bf16, name="features")
+        nc.sync.dma_start(features[:], table)
+        weights = held.tile([P, M], bf16, name="weights")
+        nc.scalar.dma_start(weights[:], w)
+        bias = held.tile([P, BLOCKS], f32, name="bias")
+        nc.scalar.dma_start(bias[:], b.rearrange("(a p) o -> p (a o)", p=P))
+
+        result = held.tile([P, BLOCKS, V], f32, name="result")
+        for a in range(BLOCKS):
+            total = sums.tile([P, V], f32, name="total")
+            for t in range(T):
+                neighbours = features[:].indirect(offsets[:, t * PIECE : (t + 1) * PIECE])
+                nc.tensor.matmul(
+                    total[:], weights[:, a * P : (a + 1) * P], neighbours, start=t == 0, stop=t == T - 1
+                )
+            nc.vector.tensor_scalar(result[:, a, :], total[:], bias[:, a : a + 1], 0.0, add, largest)
+        nc.sync.dma_start(out.rearrange("(a p) v -> p a v", p=P), result[:])

@@ -27,7 +27,8 @@ def tile_gather_matmul_kernel(tc, table, w, b, offs, out):
         weights = held.tile([P, M], bf16, name="weights")
         nc.scalar.dma_start(weights[:], w)
         bias = held.tile([P, BLOCKS], f32, name="bias")
-        nc.scalar.dma_start(bias[:], b.rearrange("(a p) o -> p (a o)", p=P))
+        nc.scalar.dma_start(bias[:], b.rearrange("(p a) o -> p (a o)", a=BLOCKS))
+        weights_of_block = weights[:].rearrange("k (p a) -> k a p", a=BLOCKS)
 
         result = held.tile([P, BLOCKS, V], f32, name="result")
         for a in range(BLOCKS):
@@ -35,7 +36,7 @@ def tile_gather_matmul_kernel(tc, table, w, b, offs, out):
             for t in range(T):
                 neighbours = features[:].indirect(offsets[:, t * PIECE : (t + 1) * PIECE])
                 nc.tensor.matmul(
-                    total[:], weights[:, a * P : (a + 1) * P], neighbours, start=t == 0, stop=t == T - 1
+                    total[:], weights_of_block[:, a, :], neighbours, start=t == 0, stop=t == T - 1
                 )
             nc.vector.tensor_scalar(result[:, a, :], total[:], bias[:, a : a + 1], 0.0, add, largest)
-        nc.sync.dma_start(out.rearrange("(a p) v -> p a v", p=P), result[:])
+        nc.sync.dma_start(out.rearrange("(p a) v -> p a v", a=BLOCKS), result[:])

@@ -5,6 +5,7 @@ M = 512
 V = 128
 T = 2
 BLOCKS = M // P
+HALVES = 2
 PIECE = V // 16
 
 FLOPS = 2 * P * M * V * T
@@ -30,13 +31,17 @@ def tile_gather_matmul_kernel(tc, table, w, b, offs, out):
         nc.scalar.dma_start(bias[:], b.rearrange("(p a) o -> p (a o)", a=BLOCKS))
         weights_of_block = weights[:].rearrange("k (p a) -> k a p", a=BLOCKS)
 
-        result = held.tile([P, BLOCKS, V], f32, name="result")
-        for a in range(BLOCKS):
-            total = sums.tile([P, V], f32, name="total")
-            for t in range(T):
-                neighbours = features[:].indirect(offsets[:, t * PIECE : (t + 1) * PIECE])
-                nc.tensor.matmul(
-                    total[:], weights_of_block[:, a, :], neighbours, start=t == 0, stop=t == T - 1
-                )
-            nc.vector.tensor_scalar(result[:, a, :], total[:], bias[:, a : a + 1], 0.0, add, largest)
-        nc.sync.dma_start(out.rearrange("(p a) v -> p a v", a=BLOCKS), result[:])
+        out_of_half = out.rearrange("(p h c) v -> h p c v", h=HALVES, c=BLOCKS // HALVES)
+        queue_of_half = (nc.sync, nc.scalar)
+        for h in range(HALVES):
+            result = held.tile([P, BLOCKS // HALVES, V], f32, name=f"result{h}")
+            for c in range(BLOCKS // HALVES):
+                a = h * (BLOCKS // HALVES) + c
+                total = sums.tile([P, V], f32, name="total")
+                for t in range(T):
+                    neighbours = features[:].indirect(offsets[:, t * PIECE : (t + 1) * PIECE])
+                    nc.tensor.matmul(
+                        total[:], weights_of_block[:, a, :], neighbours, start=t == 0, stop=t == T - 1
+                    )
+                nc.vector.tensor_scalar(result[:, c, :], total[:], bias[:, a : a + 1], 0.0, add, largest)
+            queue_of_half[h].dma_start(out_of_half[h], result[:])

import concourse.mybir as mybir

P = 128
M = 512
V = 128
T = 2
BLOCKS = M // P
HALVES = 2
PIECE = V // 16

FLOPS = 2 * P * M * V * T


def tile_gather_matmul_kernel(tc, table, w, b, offs, out):
    nc = tc.nc
    f32, bf16, u16 = mybir.dt.float32, mybir.dt.bfloat16, mybir.dt.uint16
    add, largest = mybir.AluOpType.add, mybir.AluOpType.max
    nodes = table.shape[1]

    with (
        tc.tile_pool(name="held", bufs=1) as held,
        tc.psum_pool(name="sums", bufs=BLOCKS) as sums,
    ):
        offsets = held.tile([P, T * PIECE], u16, name="offsets")
        nc.sync.dma_start(offsets[:], offs)
        features = held.tile([P, nodes], bf16, name="features")
        nc.sync.dma_start(features[:], table)
        weights = held.tile([P, M], bf16, name="weights")
        nc.scalar.dma_start(weights[:], w)
        bias = held.tile([P, BLOCKS], f32, name="bias")
        nc.scalar.dma_start(bias[:], b.rearrange("(p a) o -> p (a o)", a=BLOCKS))
        weights_of_block = weights[:].rearrange("k (p a) -> k a p", a=BLOCKS)

        out_of_half = out.rearrange("(p h c) v -> h p c v", h=HALVES, c=BLOCKS // HALVES)
        queue_of_half = (nc.sync, nc.scalar)
        for h in range(HALVES):
            result = held.tile([P, BLOCKS // HALVES, V], f32, name=f"result{h}")
            for c in range(BLOCKS // HALVES):
                a = h * (BLOCKS // HALVES) + c
                total = sums.tile([P, V], f32, name="total")
                for t in range(T):
                    neighbours = features[:].indirect(offsets[:, t * PIECE : (t + 1) * PIECE])
                    nc.tensor.matmul(
                        total[:], weights_of_block[:, a, :], neighbours, start=t == 0, stop=t == T - 1
                    )
                nc.vector.tensor_scalar(result[:, c, :], total[:], bias[:, a : a + 1], 0.0, add, largest)
            queue_of_half[h].dma_start(out_of_half[h], result[:])
